import numpy as np
import ml_dtypes


def mxq(x, axis, fmt="e4m3"):
    dtype, down = {"e4m3": (ml_dtypes.float8_e4m3fn, 7), "e5m2": (ml_dtypes.float8_e5m2, 14)}[fmt]
    v = np.moveaxis(np.asarray(x, np.float32).astype(ml_dtypes.bfloat16).astype(np.float64), axis, -1)
    blocks = v.reshape(v.shape[:-1] + (-1, 32))
    amax = np.abs(blocks).max(-1, keepdims=True)
    byte = np.maximum(np.where(amax > 0, np.frexp(amax)[1] - 1 + 127, 0) - down, 1)
    scale = np.exp2(byte - 127.0)
    codes = (blocks / scale).astype(np.float32).astype(dtype).astype(np.float64)
    return np.moveaxis((codes * scale).reshape(v.shape), -1, axis)


WIDE = False


def mx_kscale(k):
    if not WIDE:
        return np.ones(k)
    levels = np.array([10, -10, 5, -5, 0])
    if k % 512:
        return np.exp2(np.random.permutation(np.resize(levels, k // 32))).repeat(32)
    a = np.empty((k // 512, 16))
    for p in range(k // 512):
        a[p, :8] = np.random.permutation(np.resize(levels, 8))
        for g in range(8):
            far = levels[np.abs(levels - a[p, g]) >= 10]
            a[p, g + 8] = far[np.random.randint(len(far))]
    return np.exp2(a.ravel()).repeat(32)


def f64(x):
    return np.asarray(x).astype(np.float64)


def striped(idx):
    return np.tile(idx.reshape(-1, 16).T, (8, 1)).astype(np.uint16)


def unstriped(offs):
    return offs[:16].T.reshape(-1).astype(np.int64)


E2M1 = np.array([0.0, 0.5, 1.0, 1.5, 2.0, 3.0, 4.0, 6.0, -0.0, -0.5, -1.0, -1.5, -2.0, -3.0, -4.0, -6.0])


def pack_weight(w, fmt):
    k, n = w.shape
    w = f64(np.asarray(w, np.float32).astype(ml_dtypes.bfloat16)).reshape(k // 32, 32, n)
    amax = np.abs(w).max(1)
    if fmt == "e4m3":
        byte = np.frexp(amax)[1] - 1 + 127 - 7
    else:
        mant, ex = np.frexp(amax / 6.0)
        byte = np.where(mant > 0.5, ex, ex - 1) + 127
    byte = np.clip(np.where(amax > 0, byte, 1), 1, 254)
    scaled = (w * np.exp2(127.0 - byte)[:, None, :]).reshape(k, n).astype(np.float32)
    by_word = np.ascontiguousarray(scaled.reshape(k // 512, 128, 4, n).transpose(0, 1, 3, 2))
    if fmt == "e4m3":
        words = by_word.astype(ml_dtypes.float8_e4m3fn).view(np.uint8)
    else:
        c = by_word.astype(ml_dtypes.float4_e2m1fn).view(np.uint8) & 0xF
        words = (c[..., 0::2] | (c[..., 1::2] << 4)).reshape(k // 512, 128, 2 * n)
    return np.ascontiguousarray(words), np.ascontiguousarray(byte.astype(np.uint8).reshape(k // 512, 16, n))


def unpack_weight(words, scales, fmt):
    g, _, n = scales.shape
    words = np.ascontiguousarray(words).reshape(g, 128, n, -1)
    if fmt == "e4m3":
        vals = words.view(ml_dtypes.float8_e4m3fn).astype(np.float64)
    else:
        nib = np.empty((g, 128, n, 4), np.uint8)
        nib[..., 0::2] = words & 0xF
        nib[..., 1::2] = words >> 4
        vals = E2M1[nib]
    vals = vals * np.repeat(np.exp2(scales.astype(np.float64) - 127.0), 8, axis=1)[..., None]
    return vals.transpose(0, 1, 3, 2).reshape(g * 512, n)


def gelu(v):
    return 0.5 * v * (1.0 + np.tanh(np.sqrt(2.0 / np.pi) * (v + 0.044715 * v**3)))


K, K2, T, TB, S, P, H, N = 1024, 512, 4096, 2048, 1024, 512, 1024, 512

def setup_inputs():
    n = np.random.standard_normal
    s, s2, u = mx_kscale(K)[:, None], mx_kscale(K2)[:, None], mx_kscale(H)[:, None]
    d = {}
    d["tab_words"], d["tab_scales"] = pack_weight(n((K, T)) * s, "e4m3")
    d["tab2_words"], d["tab2_scales"] = pack_weight(n((K2, TB)) * s2, "e4m3")
    d["offs"] = striped(np.random.permutation(T)[:S])
    d["offs2"] = striped(np.random.permutation(TB)[:P])
    d["pos1"] = striped(np.random.permutation(S)[:P])
    d["w1_words"], d["w1_scales"] = pack_weight(n((K, H)) / K**0.5 / s * u.T, "e4m3")
    d["w2"] = (n((K2, H)) / K2**0.5 / s2 * u.T).astype(np.float32)
    d["w3"] = (n((K2, H)) / K2**0.5 / s2 * u.T).astype(np.float32)
    d["th"] = ((0.8 + 0.6 * n(H)) * u[:, 0]).astype(np.float32)
    d["wgs"] = np.exp(0.3 * n((128, P))).astype(np.float32)
    d["w4_words"], d["w4_scales"] = pack_weight(n((H, N)) / H**0.5 / u, "e2m1")
    d["w5"] = (n((H, N)) / H**0.5 / u).astype(np.float32)
    return d

def reference(tab_words, tab_scales, tab2_words, tab2_scales, offs, offs2, pos1,
              w1_words, w1_scales, w2, w3, th, wgs, w4_words, w4_scales, w5):
    v = unpack_weight(tab_words, tab_scales, "e4m3")[:, unstriped(offs)]
    v2 = unpack_weight(tab2_words, tab2_scales, "e4m3")[:, unstriped(offs2)]
    w1 = unpack_weight(w1_words, w1_scales, "e4m3")
    w4 = unpack_weight(w4_words, w4_scales, "e2m1")
    a = np.abs(w1.T @ v) - f64(th)[:, None]
    b2 = mxq(f64(w2), 0, "e4m3").T @ v2
    b3 = mxq(f64(w3), 0, "e4m3").T @ v2
    b = np.minimum(b2, b3)
    placed = np.zeros((H, S))
    placed[:, unstriped(pos1)] = np.tile(f64(wgs), (H // 128, 1)) * b
    z = mxq(a - placed, 0, "e4m3")
    y4 = w4.T @ z
    y5 = mxq(f64(w5), 0, "e4m3").T @ z
    return y4 * y5

@@ -1,0 +1,410 @@
+from contextlib import ExitStack
+
+import concourse.mybir as mybir
+from concourse.masks import make_identity
+
+K, K2, T, TB, S, PL, H, N = 1024, 512, 4096, 2048, 1024, 512, 1024, 512
+FLOPS = 2 * (K * H * S + 2 * K2 * H * PL + 2 * H * N * S)
+
+F32 = mybir.dt.float32
+BF16 = mybir.dt.bfloat16
+I32 = mybir.dt.int32
+U32 = mybir.dt.uint32
+U16 = mybir.dt.uint16
+U8 = mybir.dt.uint8
+FP8X4 = mybir.dt.float8_e4m3fn_x4
+FP4X4 = mybir.dt.float4_e2m1fn_x4
+ALU = mybir.AluOpType
+ACT = mybir.ActivationFunctionType
+
+P = 128
+HALF = 512
+VECTOR_SHARE = (320, 0)
+B2_BANKS = ("b0", "b1", "b2", "b3", "z0", "z1", "b0", "b1")
+PAGE_OF = (0, 1, 2, 3, 0, 1, 0, 0)
+
+
+def tile_list_dispatch_urgency_scores_kernel(
+    tc, tab_words, tab_scales, tab2_words, tab2_scales, offs, offs2, pos1,
+    w1_words, w1_scales, w2, w3, th, wgs, w4_words, w4_scales, w5, out,
+):
+    nc = tc.nc
+    with ExitStack() as ctx:
+        lists = ctx.enter_context(tc.tile_pool(name="lists", bufs=1))
+        keep = ctx.enter_context(tc.tile_pool(name="keep", bufs=1))
+        ring = ctx.enter_context(tc.tile_pool(name="ring", bufs=2))
+        psum = ctx.enter_context(tc.psum_pool(name="psum", bufs=1))
+
+        def kept(shape, dtype, name):
+            return keep.tile(shape, dtype, name=name, align_bytes=64)
+
+        def ringed(shape, dtype, tag, bufs):
+            return ring.tile(shape, dtype, name=tag, tag=tag, bufs=bufs, align_bytes=64)
+
+        def bank(tag):
+            return psum.tile([P, HALF], F32, name=tag, tag=tag)
+
+        def load_list(src, name):
+            dst = lists.tile(list(src.shape), U16, name=name)
+            nc.sync.dma_start(dst[:], src)
+            return dst
+
+        def zeroed_plane(engine, shape, name):
+            plane = kept(shape, U8, name)
+            engine.memset(plane[:].bitcast(I32), 0)
+            return plane
+
+        def load_stacked_scales(queue, plane, src):
+            passes = src.shape[0]
+            for q in range(4):
+                queue.dma_start(
+                    plane[32 * q : 32 * q + 4 * passes, :].bitcast(I32),
+                    src[:, 4 * q : 4 * q + 4, :].bitcast(I32),
+                )
+
+        def words_of(src):
+            return src.rearrange("p c i -> p (c i)").bitcast(I32)
+
+        def load_rows(dst, src):
+            nc.sync.dma_start(dst[:], src.rearrange("(p j) c -> p j c", j=4))
+
+        def cast(engine, dst, src):
+            if engine == "vector":
+                nc.vector.tensor_copy(dst, src)
+            else:
+                nc.scalar.activation(dst, src, ACT.Copy)
+
+        def interleave(engine, dst, src):
+            cast(
+                engine,
+                dst.rearrange("p (c i j) -> p c j i", i=4, j=4),
+                src.rearrange("p j (c i) -> p c j i", i=4),
+            )
+
+        def quantize(grouped, name):
+            width = grouped.shape[1] // 4
+            codes = kept([P, width], U32, name + "_codes")
+            scales = kept([P, width], U8, name + "_scales")
+            nc.vector.quantize_mx(codes[:].bitcast(FP8X4), scales[:], grouped)
+            return codes, scales
+
+        tab2_plane = zeroed_plane(nc.vector, [P, TB], "tab2_plane")
+        tab_plane = zeroed_plane(nc.vector, [P, T], "tab_plane")
+        w1_plane = zeroed_plane(nc.vector, [P, H], "w1_plane")
+        w4_plane = zeroed_plane(nc.vector, [P, 2 * N], "w4_plane")
+        pages = [kept([P, S], F32, f"page{i}") for i in range(4)]
+        for page in pages:
+            nc.gpsimd.memset(page[:], 0.0)
+        ident = kept([P, P], F32, "ident")
+        make_identity(nc, ident[:])
+
+        idx2 = load_list(offs2, "idx2")
+        load_stacked_scales(nc.sync, tab2_plane, tab2_scales)
+        chunks = ((0, 128), (128, 128), (256, 256))
+        raw_low = {}
+
+        def load_low(c):
+            c0, width = chunks[c]
+            for m, w in enumerate((w2, w3)):
+                raw_low[c, m] = kept([P, 4, width], F32, f"raw_low{c}_{m}")
+                load_rows(raw_low[c, m], w[:, c0 : c0 + width])
+
+        def load_high(w, tag):
+            raw = ringed([P, 4, HALF], F32, tag, 1)
+            load_rows(raw, w[:, HALF:H])
+            return raw
+
+        load_low(0)
+        seat = load_list(pos1, "seat")
+        tab2_sb = kept([P, TB], U32, "tab2_sb")
+        nc.sync.dma_start(tab2_sb[:].bitcast(I32), words_of(tab2_words[0]))
+        load_low(1)
+        wgs_rows = kept([P, PL], F32, "wgs_rows")
+        nc.sync.dma_start(wgs_rows[:], wgs)
+        tab_sb = [ringed([P, T], U32, f"tab_sb{a}", 1) for a in range(2)]
+        idx = load_list(offs, "idx")
+        load_low(2)
+        load_stacked_scales(nc.sync, tab_plane, tab_scales)
+        raw_high = [load_high(w2, "raw_w2"), load_high(w3, "raw_w3")]
+        nc.sync.dma_start(tab_sb[0][:].bitcast(I32), words_of(tab_words[0]))
+        nc.sync.dma_start(tab_sb[1][:].bitcast(I32), words_of(tab_words[1]))
+        w1_bytes = w1_words.rearrange("a p c i -> p a (c i)")
+        w1_low = kept([P, 2, HALF], I32, "w1_low")
+        nc.sync.dma_start(w1_low[:], w1_bytes[:, :, 0 : 4 * HALF].bitcast(I32))
+        load_stacked_scales(nc.sync, w1_plane, w1_scales)
+        th_low = kept([P, 4], F32, "th_low")
+        with nc.allow_non_contiguous_dma(reason="one level for each partition"):
+            nc.sync.dma_start(th_low[:], th[0:HALF].rearrange("(i p) -> p i", p=P))
+        th_high = kept([P, 4], F32, "th_high")
+        nc.sync.dma_start(th_high[:], th[HALF:H].rearrange("(p t) -> p t", t=4))
+        w1_high = kept([P, 2, HALF], I32, "w1_high")
+        nc.sync.dma_start(w1_high[:], w1_bytes[:, :, 4 * HALF : 4 * H].bitcast(I32))
+        wgs_dealt = [kept([P, PL], F32, f"wgs_dealt{t}") for t in range(4)]
+
+        def load_dealt(t):
+            for q in range(4):
+                nc.sync.dma_start(wgs_dealt[t][32 * q : 32 * q + 32, :], wgs.rearrange("(p t) j -> p t j", t=4)[:, t, :])
+
+        def load_w4():
+            for q in range(4):
+                nc.sync.dma_start(
+                    w4_plane[32 * q : 32 * q + 4, :].bitcast(I32).rearrange("r (a n) -> r a n", a=2),
+                    w4_scales[:, 4 * q : 4 * q + 4, :].bitcast(I32).rearrange("a r n -> r a n"),
+                )
+            words = kept([P, 2, 2 * N], U8, "w4_sb")
+            nc.sync.dma_start(words[:].bitcast(I32), w4_words.rearrange("a p c -> p a c").bitcast(I32))
+            return words
+
+        v2_scales = kept([P, PL], U8, "v2_scales")
+        nc.vector.tensor_copy(v2_scales[:], tab2_plane[:].indirect(idx2[:]))
+        weights = {}
+
+        def prepare_low(c):
+            c0, width = chunks[c]
+            grouped = ringed([P, 8 * width], BF16, "grouped", 3)
+            for m in range(2):
+                engine = "vector" if (c, m) == (0, 1) else "scalar"
+                interleave(engine, grouped[:, 4 * width * m : 4 * width * (m + 1)], raw_low[c, m][:])
+            codes, scales = quantize(grouped[:], f"w23_low{c}")
+            for i in range(width // P):
+                for m in range(2):
+                    cols = slice(width * m + P * i, width * m + P * (i + 1))
+                    weights[c0 // P + i, m] = (codes[:, cols], scales[:, cols])
+
+        def prepare_high():
+            for m in range(2):
+                grouped = ringed([P, 4 * HALF], BF16, "grouped", 3)
+                cast(
+                    "scalar",
+                    grouped[:].rearrange("p (t q j) -> p q j t", t=4, j=4),
+                    raw_high[m][:].rearrange("p j (q t) -> p q j t", t=4),
+                )
+                codes, scales = quantize(grouped[:], f"w23_high{m}")
+                for t in range(4):
+                    cols = slice(P * t, P * (t + 1))
+                    weights[4 + t, m] = (codes[:, cols], scales[:, cols])
+
+        prepare_low(0)
+        v2 = kept([P, PL], U32, "v2")
+        nc.vector.tensor_copy(v2[:], tab2_sb[:].indirect(idx2[:]))
+        smaller = {}
+        reused = []
+        after_casts = []
+
+        def callback_views(i):
+            views = []
+            for m in (1, 0):
+                acc = bank(f"a{i % 2}" if m else B2_BANKS[i])
+                codes, scales = weights[i, m]
+                nc.tensor.matmul_mx(
+                    acc[:], lhsT=codes.bitcast(FP8X4), lhsT_scale=scales,
+                    rhs=v2[:].bitcast(FP8X4), rhs_scale=v2_scales[:], start=True, stop=True,
+                )
+                views.append(acc)
+            if i < 2:
+                minus_b3 = kept([P, PL], F32, f"minus_b3_{i}")[:]
+                smaller[i] = kept([P, PL], F32, f"minus_b_{i}")[:]
+            else:
+                minus_b3 = after_casts[(i - 2) // 4][:, (i - 2) % 4, :]
+                smaller[i] = reused[1][:, PL * (i - 2) : PL * (i - 1)] if i < 4 else reused[0][:, PL * (i - 4) : PL * (i - 3)]
+            nc.scalar.activation(minus_b3, views[0][:], ACT.Copy, scale=-1.0)
+            nc.vector.scalar_tensor_tensor(
+                smaller[i], views[1][:], -1.0, minus_b3, ALU.mult, ALU.max
+            )
+
+        def place(i):
+            gain = wgs_rows[:] if i < 4 else wgs_dealt[i - 4][:]
+            nc.vector.tensor_tensor(pages[PAGE_OF[i]][:].indirect(seat[:]), smaller[i], gain, ALU.mult)
+
+        callback_views(0)
+        place(0)
+
+        prepare_low(1)
+        callback_views(1)
+        place(1)
+        prepare_low(2)
+        prepare_high()
+        after_casts.extend(ringed([P, 4, PL], F32, tag, 1) for tag in ("raw_w3", "raw_w2"))
+        v_scales = kept([P, S], U8, "v_scales")
+        nc.vector.tensor_copy(v_scales[:], tab_plane[:].indirect(idx[:]))
+        v = [kept([P, S], U32, f"v{a}") for a in range(2)]
+        for a in range(2):
+            nc.vector.tensor_copy(v[a][:], tab_sb[a][:].indirect(idx[:]))
+        reused.extend(ringed([P, T], F32, f"tab_sb{a}", 1) for a in range(2))
+        minus_th_low = kept([P, 4], F32, "minus_th_low")
+        nc.gpsimd.tensor_scalar(minus_th_low[:], th_low[:], -1.0, 0.0, ALU.mult, ALU.add)
+
+        for i in (2, 3):
+            callback_views(i)
+            place(i)
+        for i in range(4, 8):
+            callback_views(i)
+
+        w1_dealt = kept([P, 2, HALF], I32, "w1_dealt")
+        nc.vector.tensor_copy(
+            w1_dealt[:].rearrange("p a (t q) -> p a q t", t=4),
+            w1_high[:].rearrange("p a (q t) -> p a q t", t=4),
+        )
+        w1_plane_dealt = kept([P, HALF], U8, "w1_plane_dealt")
+        nc.vector.tensor_copy(
+            w1_plane_dealt[:].rearrange("p (t q) -> p t q", t=4),
+            w1_plane[:, HALF:H].rearrange("p (q t) -> p t q", t=4),
+        )
+
+        raw_w5 = []
+        for a in range(2):
+            raw = ringed([P, 4, N], F32, ("raw_w3", "raw_w2")[a], 1)
+            load_dealt(a)
+            load_rows(raw, w5[HALF * a : HALF * (a + 1), :])
+            raw_w5.append(raw)
+        load_dealt(2)
+        w4_sb = load_w4()
+        load_dealt(3)
+
+        def magnitudes(i):
+            words, plane = (w1_low, w1_plane) if i < 4 else (w1_dealt, w1_plane_dealt)
+            cols = slice(P * (i % 4), P * (i % 4 + 1))
+            size = reused[(i - 4) // 2][:, S * (2 + i % 2) : S * (3 + i % 2)] if i >= 4 else ringed([P, S], F32, "size", 3)[:]
+            for h in range(2):
+                seats = slice(HALF * h, HALF * (h + 1))
+                acc = bank(f"a{h}")
+                for a in range(2):
+                    nc.tensor.matmul_mx(
+                        acc[:], lhsT=words[:, a, cols].bitcast(FP8X4), lhsT_scale=plane[4 * a :, cols],
+                        rhs=v[a][:, seats].bitcast(FP8X4), rhs_scale=v_scales[4 * a :, seats],
+                        start=a == 0, stop=a == 1,
+                    )
+                nc.scalar.activation(size[:, seats], acc[:], ACT.Abs)
+            return size
+
+        z_turned = [kept([P, 4, HALF], BF16, f"z_turned{h}") for h in range(2)]
+
+        def sum_turned(i, size):
+            level = minus_th_low[:, i : i + 1].to_broadcast([P, P])
+            for h in range(2):
+                acc = bank(f"z{h}")
+                for term in range(3):
+                    for b in range(4):
+                        seats = slice(HALF * h + P * b, HALF * h + P * (b + 1))
+                        src = (size[:, seats], level, pages[i][:, seats])[term]
+                        nc.tensor.matmul(
+                            acc[:, P * b : P * (b + 1)], lhsT=src, rhs=ident[:], is_transpose=True,
+                            start=(term, b) == (0, 0), stop=(term, b) == (2, 3),
+                        )
+                nc.scalar.copy(
+                    z_turned[h][:].rearrange("j b (u q e) -> j b u q e", u=2, e=2)[:, :, :, 32 * i : 32 * (i + 1), :],
+                    acc[:].rearrange("j (b q u e) -> j b u q e", b=4, u=2, e=2),
+                )
+
+        z = {}
+
+        def quantize_low():
+            for h in range(2):
+                pairs = z_turned[h][:].bitcast(F32)
+                grouped = ringed([P, 2 * HALF], F32, "z_grouped", 2)
+                for g in range(2):
+                    acc = bank(f"z{g}")
+                    for b in range(2):
+                        for u in range(2):
+                            nc.tensor.transpose(
+                                acc[:, P * (2 * b + u) : P * (2 * b + u + 1)],
+                                pairs[:, 2 * g + b, P * u : P * (u + 1)], ident[:],
+                            )
+                    nc.scalar.copy(
+                        grouped[:, HALF * g : HALF * (g + 1)].rearrange("p (b j u) -> p b j u", b=2, u=2),
+                        acc[:].rearrange("p (b u j) -> p b j u", b=2, u=2),
+                    )
+                z[0, h] = quantize(grouped[:].bitcast(BF16), f"z0{h}")
+
+        z_rows = [kept([P, 4, HALF], BF16, f"z_rows{h}") for h in range(2)]
+
+        def sum_in_place(i, size):
+            t = i - 4
+            for h in range(2):
+                seats = slice(HALF * h, HALF * (h + 1))
+                nc.vector.scalar_tensor_tensor(
+                    z_rows[h][:, t, :], size[:, seats], th_high[:, t : t + 1], pages[PAGE_OF[i]][:, seats],
+                    ALU.subtract, ALU.add,
+                )
+
+        w5_q = []
+
+        def prepare_w5(a):
+            grouped = ringed([P, 4 * N], BF16, "grouped", 3)
+            interleave("scalar", grouped[:], raw_w5[a][:])
+            w5_q.append(quantize(grouped[:], f"w5_{a}"))
+
+        sizes = [magnitudes(0), magnitudes(1)]
+        sum_turned(0, sizes[0])
+        place(4)
+        sizes.append(magnitudes(2))
+        sum_turned(1, sizes[1])
+        prepare_w5(0)
+        place(5)
+        sizes.append(magnitudes(3))
+        sum_turned(2, sizes[2])
+        sizes.append(magnitudes(4))
+        sum_in_place(4, sizes[4])
+        sum_turned(3, sizes[3])
+        prepare_w5(1)
+        place(6)
+        sizes.append(magnitudes(5))
+        quantize_low()
+        sum_in_place(5, sizes[5])
+        sizes.append(magnitudes(6))
+        sum_in_place(6, sizes[6])
+        place(7)
+        sum_in_place(7, magnitudes(7))
+
+        y_banks = (("b0", "b1"), ("b2", "b3"), ("z0", "z1"), ("a0", "a1"))
+
+        def y_pass(acc4, acc5, n, h, a, which):
+            codes, scales = z[a, h]
+            if which == 4:
+                nc.tensor.matmul_mx(
+                    acc4[:], lhsT=w4_sb[:, a, 2 * P * n : 2 * P * (n + 1)].bitcast(FP4X4),
+                    lhsT_scale=w4_plane[:, N * a + P * n : N * a + P * (n + 1)],
+                    rhs=codes[:].bitcast(FP8X4), rhs_scale=scales[:], start=a == 0, stop=a == 1,
+                )
+            else:
+                cols = slice(P * n, P * (n + 1))
+                nc.tensor.matmul_mx(
+                    acc5[:], lhsT=w5_q[a][0][:, cols].bitcast(FP8X4), lhsT_scale=w5_q[a][1][:, cols],
+                    rhs=codes[:].bitcast(FP8X4), rhs_scale=scales[:], start=a == 0, stop=a == 1,
+                )
+
+        def finish(acc4, acc5, n, h):
+            y4 = ringed([P, HALF], F32, "y4", 2)
+            nc.scalar.copy(y4[:], acc4[:])
+            result = ringed([P, HALF], F32, "result", 4)
+            nc.vector.tensor_tensor(result[:], acc5[:], y4[:], ALU.mult)
+            nc.sync.dma_start(out[P * n : P * (n + 1), HALF * h : HALF * (h + 1)], result[:])
+
+        early = []
+        for n in range(4):
+            accs = (bank(y_banks[n][0]), bank(y_banks[n][1]))
+            for which in (4, 5):
+                y_pass(*accs, n, 0, 0, which)
+            early.append(accs)
+
+        for h in range(2):
+            grouped = ringed([P, 4 * HALF], BF16, "z_grouped", 2)
+            cut = VECTOR_SHARE[h]
+            if cut:
+                interleave("vector", grouped[:, 0 : 4 * cut], z_rows[h][:, :, 0:cut])
+            nc.scalar.copy(
+                grouped[:, 4 * cut :].rearrange("p (c i j) -> p c j i", i=4, j=4),
+                z_rows[h][:, :, cut:].rearrange("p j (c i) -> p c j i", i=4),
+            )
+            z[1, h] = quantize(grouped[:], f"z1{h}")
+
+        for n in range(4):
+            for which in (4, 5):
+                y_pass(*early[n], n, 0, 1, which)
+            finish(*early[n], n, 0)
+        for n in range(4):
+            accs = (bank(y_banks[n][0]), bank(y_banks[n][1]))
+            for which in (4, 5):
+                for a in range(2):
+                    y_pass(*accs, n, 1, a, which)
+            finish(*accs, n, 1)

@@ -19,7 +19,7 @@ ACT = mybir.ActivationFunctionType
 
 P = 128
 HALF = 512
-VECTOR_SHARE = (320, 0)
+QUARTER = 256
 B2_BANKS = ("b0", "b1", "b2", "b3", "z0", "z1", "b0", "b1")
 PAGE_OF = (0, 1, 2, 3, 0, 1, 0, 0)
 
@@ -89,12 +89,12 @@ def tile_list_dispatch_urgency_scores_kernel(
             return codes, scales
 
         tab2_plane = zeroed_plane(nc.vector, [P, TB], "tab2_plane")
-        tab_plane = zeroed_plane(nc.vector, [P, T], "tab_plane")
+        tab_plane = zeroed_plane(nc.gpsimd, [P, T], "tab_plane")
         w1_plane = zeroed_plane(nc.vector, [P, H], "w1_plane")
         w4_plane = zeroed_plane(nc.vector, [P, 2 * N], "w4_plane")
         pages = [kept([P, S], F32, f"page{i}") for i in range(4)]
         for page in pages:
-            nc.gpsimd.memset(page[:], 0.0)
+            nc.vector.memset(page[:], 0.0)
         ident = kept([P, P], F32, "ident")
         make_identity(nc, ident[:])
 
@@ -118,13 +118,16 @@ def tile_list_dispatch_urgency_scores_kernel(
         seat = load_list(pos1, "seat")
         tab2_sb = kept([P, TB], U32, "tab2_sb")
         nc.sync.dma_start(tab2_sb[:].bitcast(I32), words_of(tab2_words[0]))
+        load_stacked_scales(nc.gpsimd, tab_plane, tab_scales)
+        idx = load_list(offs, "idx")
         load_low(1)
+        th_low = kept([P, 4], F32, "th_low")
+        with nc.allow_non_contiguous_dma(reason="one level for each partition"):
+            nc.sync.dma_start(th_low[:], th[0:HALF].rearrange("(i p) -> p i", p=P))
         wgs_rows = kept([P, PL], F32, "wgs_rows")
         nc.sync.dma_start(wgs_rows[:], wgs)
         tab_sb = [ringed([P, T], U32, f"tab_sb{a}", 1) for a in range(2)]
-        idx = load_list(offs, "idx")
         load_low(2)
-        load_stacked_scales(nc.sync, tab_plane, tab_scales)
         raw_high = [load_high(w2, "raw_w2"), load_high(w3, "raw_w3")]
         nc.sync.dma_start(tab_sb[0][:].bitcast(I32), words_of(tab_words[0]))
         nc.sync.dma_start(tab_sb[1][:].bitcast(I32), words_of(tab_words[1]))
@@ -132,9 +135,6 @@ def tile_list_dispatch_urgency_scores_kernel(
         w1_low = kept([P, 2, HALF], I32, "w1_low")
         nc.sync.dma_start(w1_low[:], w1_bytes[:, :, 0 : 4 * HALF].bitcast(I32))
         load_stacked_scales(nc.sync, w1_plane, w1_scales)
-        th_low = kept([P, 4], F32, "th_low")
-        with nc.allow_non_contiguous_dma(reason="one level for each partition"):
-            nc.sync.dma_start(th_low[:], th[0:HALF].rearrange("(i p) -> p i", p=P))
         th_high = kept([P, 4], F32, "th_high")
         nc.sync.dma_start(th_high[:], th[HALF:H].rearrange("(p t) -> p t", t=4))
         w1_high = kept([P, 2, HALF], I32, "w1_high")
@@ -232,7 +232,7 @@ def tile_list_dispatch_urgency_scores_kernel(
             nc.vector.tensor_copy(v[a][:], tab_sb[a][:].indirect(idx[:]))
         reused.extend(ringed([P, T], F32, f"tab_sb{a}", 1) for a in range(2))
         minus_th_low = kept([P, 4], F32, "minus_th_low")
-        nc.gpsimd.tensor_scalar(minus_th_low[:], th_low[:], -1.0, 0.0, ALU.mult, ALU.add)
+        nc.scalar.activation(minus_th_low[:], th_low[:], ACT.Copy, scale=-1.0)
 
         for i in (2, 3):
             callback_views(i)
@@ -261,11 +261,15 @@ def tile_list_dispatch_urgency_scores_kernel(
         w4_sb = load_w4()
         load_dealt(3)
 
-        def magnitudes(i):
+        sizes = {}
+
+        def magnitudes(i, halves=(0, 1)):
             words, plane = (w1_low, w1_plane) if i < 4 else (w1_dealt, w1_plane_dealt)
             cols = slice(P * (i % 4), P * (i % 4 + 1))
-            size = reused[(i - 4) // 2][:, S * (2 + i % 2) : S * (3 + i % 2)] if i >= 4 else ringed([P, S], F32, "size", 3)[:]
-            for h in range(2):
+            if i not in sizes:
+                sizes[i] = reused[(i - 4) // 2][:, S * (2 + i % 2) : S * (3 + i % 2)] if i >= 4 else ringed([P, S], F32, "size", 3)[:]
+            size = sizes[i]
+            for h in halves:
                 seats = slice(HALF * h, HALF * (h + 1))
                 acc = bank(f"a{h}")
                 for a in range(2):
@@ -275,13 +279,13 @@ def tile_list_dispatch_urgency_scores_kernel(
                         start=a == 0, stop=a == 1,
                     )
                 nc.scalar.activation(size[:, seats], acc[:], ACT.Abs)
-            return size
 
         z_turned = [kept([P, 4, HALF], BF16, f"z_turned{h}") for h in range(2)]
 
-        def sum_turned(i, size):
+        def sum_turned(i, halves):
+            size = sizes[i]
             level = minus_th_low[:, i : i + 1].to_broadcast([P, P])
-            for h in range(2):
+            for h in halves:
                 acc = bank(f"z{h}")
                 for term in range(3):
                     for b in range(4):
@@ -298,8 +302,8 @@ def tile_list_dispatch_urgency_scores_kernel(
 
         z = {}
 
-        def quantize_low():
-            for h in range(2):
+        def quantize_low(halves):
+            for h in halves:
                 pairs = z_turned[h][:].bitcast(F32)
                 grouped = ringed([P, 2 * HALF], F32, "z_grouped", 2)
                 for g in range(2):
@@ -316,16 +320,22 @@ def tile_list_dispatch_urgency_scores_kernel(
                     )
                 z[0, h] = quantize(grouped[:].bitcast(BF16), f"z0{h}")
 
-        z_rows = [kept([P, 4, HALF], BF16, f"z_rows{h}") for h in range(2)]
+        z_rows = [kept([P, 2, 4, QUARTER], BF16, f"z_rows{h}") for h in range(2)]
 
-        def sum_in_place(i, size):
+        def sum_in_place(i, h, quarters):
             t = i - 4
+            seats = slice(HALF * h + QUARTER * quarters.start, HALF * h + QUARTER * quarters.stop)
+            nc.vector.scalar_tensor_tensor(
+                z_rows[h][:, quarters, t, :],
+                sizes[i][:, seats].rearrange("p (g j) -> p g j", j=QUARTER),
+                th_high[:, t : t + 1],
+                pages[PAGE_OF[i]][:, seats].rearrange("p (g j) -> p g j", j=QUARTER),
+                ALU.subtract, ALU.add,
+            )
+
+        def sum_whole(i):
             for h in range(2):
-                seats = slice(HALF * h, HALF * (h + 1))
-                nc.vector.scalar_tensor_tensor(
-                    z_rows[h][:, t, :], size[:, seats], th_high[:, t : t + 1], pages[PAGE_OF[i]][:, seats],
-                    ALU.subtract, ALU.add,
-                )
+                sum_in_place(i, h, slice(0, 2))
 
         w5_q = []
 
@@ -334,77 +344,105 @@ def tile_list_dispatch_urgency_scores_kernel(
             interleave("scalar", grouped[:], raw_w5[a][:])
             w5_q.append(quantize(grouped[:], f"w5_{a}"))
 
-        sizes = [magnitudes(0), magnitudes(1)]
-        sum_turned(0, sizes[0])
-        place(4)
-        sizes.append(magnitudes(2))
-        sum_turned(1, sizes[1])
-        prepare_w5(0)
-        place(5)
-        sizes.append(magnitudes(3))
-        sum_turned(2, sizes[2])
-        sizes.append(magnitudes(4))
-        sum_in_place(4, sizes[4])
-        sum_turned(3, sizes[3])
-        prepare_w5(1)
+        magnitudes(0)
+        for i in range(4):
+            for h in range(2):
+                magnitudes(i + 1, (h,))
+                sum_turned(i, (h,))
+            if i < 2:
+                place(4 + i)
+            if i in (1, 3):
+                prepare_w5(i // 2)
+        sum_whole(4)
         place(6)
-        sizes.append(magnitudes(5))
-        quantize_low()
-        sum_in_place(5, sizes[5])
-        sizes.append(magnitudes(6))
-        sum_in_place(6, sizes[6])
+        for h in range(2):
+            magnitudes(5, (h,))
+            quantize_low((h,))
+        sum_whole(5)
+        magnitudes(6)
+        sum_whole(6)
         place(7)
-        sum_in_place(7, magnitudes(7))
+        magnitudes(7)
 
         y_banks = (("b0", "b1"), ("b2", "b3"), ("z0", "z1"), ("a0", "a1"))
 
-        def y_pass(acc4, acc5, n, h, a, which):
+        def y4_pass(acc, n, h, a, seats, stop):
             codes, scales = z[a, h]
-            if which == 4:
-                nc.tensor.matmul_mx(
-                    acc4[:], lhsT=w4_sb[:, a, 2 * P * n : 2 * P * (n + 1)].bitcast(FP4X4),
-                    lhsT_scale=w4_plane[:, N * a + P * n : N * a + P * (n + 1)],
-                    rhs=codes[:].bitcast(FP8X4), rhs_scale=scales[:], start=a == 0, stop=a == 1,
-                )
-            else:
-                cols = slice(P * n, P * (n + 1))
-                nc.tensor.matmul_mx(
-                    acc5[:], lhsT=w5_q[a][0][:, cols].bitcast(FP8X4), lhsT_scale=w5_q[a][1][:, cols],
-                    rhs=codes[:].bitcast(FP8X4), rhs_scale=scales[:], start=a == 0, stop=a == 1,
-                )
+            nc.tensor.matmul_mx(
+                acc[:, seats], lhsT=w4_sb[:, a, 2 * P * n : 2 * P * (n + 1)].bitcast(FP4X4),
+                lhsT_scale=w4_plane[:, N * a + P * n : N * a + P * (n + 1)],
+                rhs=codes[:, seats].bitcast(FP8X4), rhs_scale=scales[:, seats], start=a == 0, stop=stop,
+            )
 
-        def finish(acc4, acc5, n, h):
+        def y5_pass(acc, n, h, a, seats, stop):
+            codes, scales = z[a, h]
+            cols = slice(P * n, P * (n + 1))
+            nc.tensor.matmul_mx(
+                acc[:, seats], lhsT=w5_q[a][0][:, cols].bitcast(FP8X4), lhsT_scale=w5_q[a][1][:, cols],
+                rhs=codes[:, seats].bitcast(FP8X4), rhs_scale=scales[:, seats], start=a == 0, stop=stop,
+            )
+
+        def finish(acc4, acc5, n, h, pieces):
             y4 = ringed([P, HALF], F32, "y4", 2)
             nc.scalar.copy(y4[:], acc4[:])
-            result = ringed([P, HALF], F32, "result", 4)
-            nc.vector.tensor_tensor(result[:], acc5[:], y4[:], ALU.mult)
-            nc.sync.dma_start(out[P * n : P * (n + 1), HALF * h : HALF * (h + 1)], result[:])
+            width = HALF // pieces
+            result = ringed([P, HALF], F32, "result", 5)
+            for c0 in range(0, HALF, width):
+                seats = slice(c0, c0 + width)
+                nc.vector.tensor_tensor(result[:, seats], acc5[:, seats], y4[:, seats], ALU.mult)
+                nc.sync.dma_start(out[P * n : P * (n + 1), HALF * h + c0 : HALF * h + c0 + width], result[:, seats])
 
+        whole = slice(0, HALF)
         early = []
         for n in range(4):
-            accs = (bank(y_banks[n][0]), bank(y_banks[n][1]))
-            for which in (4, 5):
-                y_pass(*accs, n, 0, 0, which)
-            early.append(accs)
+            acc4, acc5 = bank(y_banks[n][0]), bank(y_banks[n][1])
+            y4_pass(acc4, n, 0, 0, whole, False)
+            y5_pass(acc5, n, 0, 0, whole, False)
+            early.append((acc4, acc5))
 
-        for h in range(2):
-            grouped = ringed([P, 4 * HALF], BF16, "z_grouped", 2)
-            cut = VECTOR_SHARE[h]
-            if cut:
-                interleave("vector", grouped[:, 0 : 4 * cut], z_rows[h][:, :, 0:cut])
-            nc.scalar.copy(
-                grouped[:, 4 * cut :].rearrange("p (c i j) -> p c j i", i=4, j=4),
-                z_rows[h][:, :, cut:].rearrange("p j (c i) -> p c j i", i=4),
-            )
-            z[1, h] = quantize(grouped[:], f"z1{h}")
+        def weave(engine, grouped, h, g):
+            dst = grouped.rearrange("p (c i j) -> p c j i", i=4, j=4)
+            src = z_rows[h][:, g, :, :].rearrange("p j (c i) -> p c j i", i=4)
+            if engine == "vector":
+                nc.vector.tensor_copy(dst, src)
+            else:
+                nc.scalar.copy(dst, src)
 
-        for n in range(4):
-            for which in (4, 5):
-                y_pass(*early[n], n, 0, 1, which)
-            finish(*early[n], n, 0)
-        for n in range(4):
-            accs = (bank(y_banks[n][0]), bank(y_banks[n][1]))
-            for which in (4, 5):
+        z[1, 0] = (kept([P, HALF], U32, "z10_codes"), kept([P, HALF], U8, "z10_scales"))
+        first = [kept([P, 4 * QUARTER], BF16, f"z_quarter{g}") for g in range(2)]
+        second = ringed([P, 4 * HALF], BF16, "z_grouped", 2)
+
+        def quantize_quarter(g):
+            seats = slice(QUARTER * g, QUARTER * (g + 1))
+            nc.vector.quantize_mx(z[1, 0][0][:, seats].bitcast(FP8X4), z[1, 0][1][:, seats], first[g][:])
+
+        sum_in_place(7, 0, slice(0, 1))
+        sum_in_place(7, 0, slice(1, 2))
+        weave("vector", first[0][:], 0, 0)
+        weave("scalar", first[1][:], 0, 1)
+        sum_in_place(7, 1, slice(1, 2))
+        quantize_quarter(0)
+        weave("scalar", second[:, 4 * QUARTER :], 1, 1)
+        sum_in_place(7, 1, slice(0, 1))
+        quantize_quarter(1)
+        weave("vector", second[:, 0 : 4 * QUARTER], 1, 0)
+        z[1, 1] = quantize(second[:], "z11")
+
+        for g in range(2):
+            for n in range(4):
+                acc4, acc5 = early[n]
+                for b in range(2):
+                    c0 = QUARTER * g + P * b
+                    y4_pass(acc4, n, 0, 1, slice(c0, c0 + P), (g, b) == (1, 1))
+                y5_pass(acc5, n, 0, 1, slice(QUARTER * g, QUARTER * (g + 1)), g == 1)
+                if g == 1:
+                    finish(acc4, acc5, n, 0, 1)
+        for pair in ((0,), (1,), (2, 3)):
+            accs = {n: (bank(y_banks[n][0]), bank(y_banks[n][1])) for n in pair}
+            for n in pair:
                 for a in range(2):
-                    y_pass(*accs, n, 1, a, which)
-            finish(*accs, n, 1)
+                    y4_pass(accs[n][0], n, 1, a, whole, a == 1)
+            for n in pair:
+                for a in range(2):
+                    y5_pass(accs[n][1], n, 1, a, whole, a == 1)
+                finish(*accs[n], n, 1, 2 if n == 3 else 1)

@@ -21,7 +21,7 @@ P = 128
 HALF = 512
 QUARTER = 256
 B2_BANKS = ("b0", "b1", "b2", "b3", "z0", "z1", "b0", "b1")
-PAGE_OF = (0, 1, 2, 3, 0, 1, 0, 0)
+PAGE_OF = (0, 1, 2, 3, 0, 1, 2, 2)
 
 
 def tile_list_dispatch_urgency_scores_kernel(
@@ -106,7 +106,7 @@ def tile_list_dispatch_urgency_scores_kernel(
         def load_low(c):
             c0, width = chunks[c]
             for m, w in enumerate((w2, w3)):
-                raw_low[c, m] = kept([P, 4, width], F32, f"raw_low{c}_{m}")
+                raw_low[c, m] = ringed([P, 4, width], F32, f"raw_low{c}_{m}", 1)
                 load_rows(raw_low[c, m], w[:, c0 : c0 + width])
 
         def load_high(w, tag):
@@ -116,7 +116,7 @@ def tile_list_dispatch_urgency_scores_kernel(
 
         load_low(0)
         seat = load_list(pos1, "seat")
-        tab2_sb = kept([P, TB], U32, "tab2_sb")
+        tab2_sb = ringed([P, TB], U32, "tab2_sb", 1)
         nc.sync.dma_start(tab2_sb[:].bitcast(I32), words_of(tab2_words[0]))
         load_stacked_scales(nc.gpsimd, tab_plane, tab_scales)
         idx = load_list(offs, "idx")
@@ -131,14 +131,6 @@ def tile_list_dispatch_urgency_scores_kernel(
         raw_high = [load_high(w2, "raw_w2"), load_high(w3, "raw_w3")]
         nc.sync.dma_start(tab_sb[0][:].bitcast(I32), words_of(tab_words[0]))
         nc.sync.dma_start(tab_sb[1][:].bitcast(I32), words_of(tab_words[1]))
-        w1_bytes = w1_words.rearrange("a p c i -> p a (c i)")
-        w1_low = kept([P, 2, HALF], I32, "w1_low")
-        nc.sync.dma_start(w1_low[:], w1_bytes[:, :, 0 : 4 * HALF].bitcast(I32))
-        load_stacked_scales(nc.sync, w1_plane, w1_scales)
-        th_high = kept([P, 4], F32, "th_high")
-        nc.sync.dma_start(th_high[:], th[HALF:H].rearrange("(p t) -> p t", t=4))
-        w1_high = kept([P, 2, HALF], I32, "w1_high")
-        nc.sync.dma_start(w1_high[:], w1_bytes[:, :, 4 * HALF : 4 * H].bitcast(I32))
         wgs_dealt = [kept([P, PL], F32, f"wgs_dealt{t}") for t in range(4)]
 
         def load_dealt(t):
@@ -147,7 +139,7 @@ def tile_list_dispatch_urgency_scores_kernel(
 
         def load_w4():
             for q in range(4):
-                nc.sync.dma_start(
+                nc.gpsimd.dma_start(
                     w4_plane[32 * q : 32 * q + 4, :].bitcast(I32).rearrange("r (a n) -> r a n", a=2),
                     w4_scales[:, 4 * q : 4 * q + 4, :].bitcast(I32).rearrange("a r n -> r a n"),
                 )
@@ -187,6 +179,16 @@ def tile_list_dispatch_urgency_scores_kernel(
         prepare_low(0)
         v2 = kept([P, PL], U32, "v2")
         nc.vector.tensor_copy(v2[:], tab2_sb[:].indirect(idx2[:]))
+        w1_bytes = w1_words.rearrange("a p c i -> p a (c i)")
+        w1_low = kept([P, 2, HALF], I32, "w1_low")
+        nc.sync.dma_start(w1_low[:], w1_bytes[:, :, 0 : 4 * HALF].bitcast(I32))
+        load_stacked_scales(nc.gpsimd, w1_plane, w1_scales)
+        raw_w5 = [ringed([P, 4, N], F32, "tab2_sb", 1)]
+        load_rows(raw_w5[0], w5[0:HALF, :])
+        th_high = kept([P, 4], F32, "th_high")
+        nc.sync.dma_start(th_high[:], th[HALF:H].rearrange("(p t) -> p t", t=4))
+        w1_high = kept([P, 2, HALF], I32, "w1_high")
+        nc.sync.dma_start(w1_high[:], w1_bytes[:, :, 4 * HALF : 4 * H].bitcast(I32))
         smaller = {}
         reused = []
         after_casts = []
@@ -202,8 +204,8 @@ def tile_list_dispatch_urgency_scores_kernel(
                 )
                 views.append(acc)
             if i < 2:
-                minus_b3 = kept([P, PL], F32, f"minus_b3_{i}")[:]
-                smaller[i] = kept([P, PL], F32, f"minus_b_{i}")[:]
+                minus_b3 = ringed([P, PL], F32, ("minus_b3_0", "raw_low2_1")[i], 1)[:]
+                smaller[i] = ringed([P, PL], F32, f"minus_b_{i}", 1)[:]
             else:
                 minus_b3 = after_casts[(i - 2) // 4][:, (i - 2) % 4, :]
                 smaller[i] = reused[1][:, PL * (i - 2) : PL * (i - 1)] if i < 4 else reused[0][:, PL * (i - 4) : PL * (i - 3)]
@@ -220,16 +222,19 @@ def tile_list_dispatch_urgency_scores_kernel(
         place(0)
 
         prepare_low(1)
+        prepare_low(2)
         callback_views(1)
         place(1)
-        prepare_low(2)
         prepare_high()
         after_casts.extend(ringed([P, 4, PL], F32, tag, 1) for tag in ("raw_w3", "raw_w2"))
         v_scales = kept([P, S], U8, "v_scales")
         nc.vector.tensor_copy(v_scales[:], tab_plane[:].indirect(idx[:]))
         v = [kept([P, S], U32, f"v{a}") for a in range(2)]
-        for a in range(2):
-            nc.vector.tensor_copy(v[a][:], tab_sb[a][:].indirect(idx[:]))
+        nc.vector.tensor_copy(v[0][:], tab_sb[0][:].indirect(idx[:]))
+        for h in range(2):
+            nc.vector.tensor_copy(
+                v[1][:, HALF * h : HALF * (h + 1)], tab_sb[1][:].indirect(idx[:, 32 * h : 32 * (h + 1)])
+            )
         reused.extend(ringed([P, T], F32, f"tab_sb{a}", 1) for a in range(2))
         minus_th_low = kept([P, 4], F32, "minus_th_low")
         nc.scalar.activation(minus_th_low[:], th_low[:], ACT.Copy, scale=-1.0)
@@ -242,21 +247,19 @@ def tile_list_dispatch_urgency_scores_kernel(
 
         w1_dealt = kept([P, 2, HALF], I32, "w1_dealt")
         nc.vector.tensor_copy(
-            w1_dealt[:].rearrange("p a (t q) -> p a q t", t=4),
-            w1_high[:].rearrange("p a (q t) -> p a q t", t=4),
+            w1_dealt[:].rearrange("p a (t q i) -> p a q t i", t=4, i=4),
+            w1_high[:].rearrange("p a (q i t) -> p a q t i", t=4, i=4),
         )
-        w1_plane_dealt = kept([P, HALF], U8, "w1_plane_dealt")
+        w1_plane_dealt = ringed([P, HALF], U8, "minus_b_1", 1)
         nc.vector.tensor_copy(
             w1_plane_dealt[:].rearrange("p (t q) -> p t q", t=4),
             w1_plane[:, HALF:H].rearrange("p (q t) -> p t q", t=4),
         )
 
-        raw_w5 = []
-        for a in range(2):
-            raw = ringed([P, 4, N], F32, ("raw_w3", "raw_w2")[a], 1)
-            load_dealt(a)
-            load_rows(raw, w5[HALF * a : HALF * (a + 1), :])
-            raw_w5.append(raw)
+        load_dealt(0)
+        raw_w5.append(ringed([P, 4, N], F32, "raw_w2", 1))
+        load_rows(raw_w5[1], w5[HALF:H, :])
+        load_dealt(1)
         load_dealt(2)
         w4_sb = load_w4()
         load_dealt(3)
@@ -339,9 +342,11 @@ def tile_list_dispatch_urgency_scores_kernel(
 
         w5_q = []
 
-        def prepare_w5(a):
+        def prepare_w5(a, pieces):
             grouped = ringed([P, 4 * N], BF16, "grouped", 3)
-            interleave("scalar", grouped[:], raw_w5[a][:])
+            width = N // pieces
+            for c0 in range(0, N, width):
+                interleave("scalar", grouped[:, 4 * c0 : 4 * (c0 + width)], raw_w5[a][:, :, c0 : c0 + width])
             w5_q.append(quantize(grouped[:], f"w5_{a}"))
 
         magnitudes(0)
@@ -349,12 +354,11 @@ def tile_list_dispatch_urgency_scores_kernel(
             for h in range(2):
                 magnitudes(i + 1, (h,))
                 sum_turned(i, (h,))
-            if i < 2:
+            if i < 3:
                 place(4 + i)
-            if i in (1, 3):
-                prepare_w5(i // 2)
+        for a in range(2):
+            prepare_w5(a, 4)
         sum_whole(4)
-        place(6)
         for h in range(2):
             magnitudes(5, (h,))
             quantize_low((h,))

@@ -92,14 +92,19 @@ def tile_list_dispatch_urgency_scores_kernel(
         tab_plane = zeroed_plane(nc.gpsimd, [P, T], "tab_plane")
         w1_plane = zeroed_plane(nc.vector, [P, H], "w1_plane")
         w4_plane = zeroed_plane(nc.vector, [P, 2 * N], "w4_plane")
-        pages = [kept([P, S], F32, f"page{i}") for i in range(4)]
-        for page in pages:
-            nc.vector.memset(page[:], 0.0)
+        pages = [kept([P, S], F32, "page0")]
+        nc.vector.memset(pages[0][:], 0.0)
+
+        def open_page(tag):
+            pages.append(ringed([P, S], F32, tag, 1))
+            nc.gpsimd.memset(pages[-1][:], 0.0)
+
+        th_rows = kept([P, P], F32, "th_rows")
+        nc.vector.memset(th_rows[:], 0.0)
         ident = kept([P, P], F32, "ident")
         make_identity(nc, ident[:])
 
         idx2 = load_list(offs2, "idx2")
-        load_stacked_scales(nc.sync, tab2_plane, tab2_scales)
         chunks = ((0, 128), (128, 128), (256, 256))
         raw_low = {}
 
@@ -114,20 +119,19 @@ def tile_list_dispatch_urgency_scores_kernel(
             load_rows(raw, w[:, HALF:H])
             return raw
 
-        load_low(0)
-        seat = load_list(pos1, "seat")
         tab2_sb = ringed([P, TB], U32, "tab2_sb", 1)
         nc.sync.dma_start(tab2_sb[:].bitcast(I32), words_of(tab2_words[0]))
+        load_stacked_scales(nc.sync, tab2_plane, tab2_scales)
+        load_low(0)
         load_stacked_scales(nc.gpsimd, tab_plane, tab_scales)
         idx = load_list(offs, "idx")
         load_low(1)
-        th_low = kept([P, 4], F32, "th_low")
-        with nc.allow_non_contiguous_dma(reason="one level for each partition"):
-            nc.sync.dma_start(th_low[:], th[0:HALF].rearrange("(i p) -> p i", p=P))
+        seat = load_list(pos1, "seat")
         wgs_rows = kept([P, PL], F32, "wgs_rows")
         nc.sync.dma_start(wgs_rows[:], wgs)
         tab_sb = [ringed([P, T], U32, f"tab_sb{a}", 1) for a in range(2)]
         load_low(2)
+        nc.sync.dma_start(th_rows[0:4, :], th[0:HALF].rearrange("(i p) -> i p", p=P))
         raw_high = [load_high(w2, "raw_w2"), load_high(w3, "raw_w3")]
         nc.sync.dma_start(tab_sb[0][:].bitcast(I32), words_of(tab_words[0]))
         nc.sync.dma_start(tab_sb[1][:].bitcast(I32), words_of(tab_words[1]))
@@ -139,7 +143,7 @@ def tile_list_dispatch_urgency_scores_kernel(
 
         def load_w4():
             for q in range(4):
-                nc.gpsimd.dma_start(
+                nc.sync.dma_start(
                     w4_plane[32 * q : 32 * q + 4, :].bitcast(I32).rearrange("r (a n) -> r a n", a=2),
                     w4_scales[:, 4 * q : 4 * q + 4, :].bitcast(I32).rearrange("a r n -> r a n"),
                 )
@@ -182,7 +186,7 @@ def tile_list_dispatch_urgency_scores_kernel(
         w1_bytes = w1_words.rearrange("a p c i -> p a (c i)")
         w1_low = kept([P, 2, HALF], I32, "w1_low")
         nc.sync.dma_start(w1_low[:], w1_bytes[:, :, 0 : 4 * HALF].bitcast(I32))
-        load_stacked_scales(nc.gpsimd, w1_plane, w1_scales)
+        load_stacked_scales(nc.sync, w1_plane, w1_scales)
         raw_w5 = [ringed([P, 4, N], F32, "tab2_sb", 1)]
         load_rows(raw_w5[0], w5[0:HALF, :])
         th_high = kept([P, 4], F32, "th_high")
@@ -219,25 +223,27 @@ def tile_list_dispatch_urgency_scores_kernel(
             nc.vector.tensor_tensor(pages[PAGE_OF[i]][:].indirect(seat[:]), smaller[i], gain, ALU.mult)
 
         callback_views(0)
+        open_page("minus_b3_0")
         place(0)
+        open_page("minus_b_0")
 
         prepare_low(1)
         prepare_low(2)
         callback_views(1)
+        open_page("raw_low2_1")
         place(1)
         prepare_high()
         after_casts.extend(ringed([P, 4, PL], F32, tag, 1) for tag in ("raw_w3", "raw_w2"))
         v_scales = kept([P, S], U8, "v_scales")
         nc.vector.tensor_copy(v_scales[:], tab_plane[:].indirect(idx[:]))
         v = [kept([P, S], U32, f"v{a}") for a in range(2)]
-        nc.vector.tensor_copy(v[0][:], tab_sb[0][:].indirect(idx[:]))
-        for h in range(2):
-            nc.vector.tensor_copy(
-                v[1][:, HALF * h : HALF * (h + 1)], tab_sb[1][:].indirect(idx[:, 32 * h : 32 * (h + 1)])
-            )
+        for a in range(2):
+            nc.vector.tensor_copy(v[a][:], tab_sb[a][:].indirect(idx[:]))
         reused.extend(ringed([P, T], F32, f"tab_sb{a}", 1) for a in range(2))
         minus_th_low = kept([P, 4], F32, "minus_th_low")
-        nc.scalar.activation(minus_th_low[:], th_low[:], ACT.Copy, scale=-1.0)
+        turned = bank("z1")
+        nc.tensor.transpose(turned[:, 0:P], th_rows[:], ident[:])
+        nc.scalar.activation(minus_th_low[:], turned[:, 0:4], ACT.Copy, scale=-1.0)
 
         for i in (2, 3):
             callback_views(i)
@@ -250,7 +256,7 @@ def tile_list_dispatch_urgency_scores_kernel(
             w1_dealt[:].rearrange("p a (t q i) -> p a q t i", t=4, i=4),
             w1_high[:].rearrange("p a (q i t) -> p a q t i", t=4, i=4),
         )
-        w1_plane_dealt = ringed([P, HALF], U8, "minus_b_1", 1)
+        w1_plane_dealt = kept([P, HALF], U8, "w1_plane_dealt")
         nc.vector.tensor_copy(
             w1_plane_dealt[:].rearrange("p (t q) -> p t q", t=4),
             w1_plane[:, HALF:H].rearrange("p (q t) -> p t q", t=4),
@@ -323,22 +329,18 @@ def tile_list_dispatch_urgency_scores_kernel(
                     )
                 z[0, h] = quantize(grouped[:].bitcast(BF16), f"z0{h}")
 
-        z_rows = [kept([P, 2, 4, QUARTER], BF16, f"z_rows{h}") for h in range(2)]
+        z_rows = kept([P, 4, 4, QUARTER], BF16, "z_rows")
 
-        def sum_in_place(i, h, quarters):
+        def sum_in_place(i, quarters):
             t = i - 4
-            seats = slice(HALF * h + QUARTER * quarters.start, HALF * h + QUARTER * quarters.stop)
+            seats = slice(QUARTER * quarters.start, QUARTER * quarters.stop)
             nc.vector.scalar_tensor_tensor(
-                z_rows[h][:, quarters, t, :],
+                z_rows[:, quarters, t, :],
                 sizes[i][:, seats].rearrange("p (g j) -> p g j", j=QUARTER),
                 th_high[:, t : t + 1],
                 pages[PAGE_OF[i]][:, seats].rearrange("p (g j) -> p g j", j=QUARTER),
                 ALU.subtract, ALU.add,
             )
-
-        def sum_whole(i):
-            for h in range(2):
-                sum_in_place(i, h, slice(0, 2))
 
         w5_q = []
 
@@ -358,13 +360,13 @@ def tile_list_dispatch_urgency_scores_kernel(
                 place(4 + i)
         for a in range(2):
             prepare_w5(a, 4)
-        sum_whole(4)
+        sum_in_place(4, slice(0, 4))
         for h in range(2):
             magnitudes(5, (h,))
             quantize_low((h,))
-        sum_whole(5)
+        sum_in_place(5, slice(0, 4))
         magnitudes(6)
-        sum_whole(6)
+        sum_in_place(6, slice(0, 4))
         place(7)
         magnitudes(7)
 
@@ -406,7 +408,7 @@ def tile_list_dispatch_urgency_scores_kernel(
 
         def weave(engine, grouped, h, g):
             dst = grouped.rearrange("p (c i j) -> p c j i", i=4, j=4)
-            src = z_rows[h][:, g, :, :].rearrange("p j (c i) -> p c j i", i=4)
+            src = z_rows[:, 2 * h + g, :, :].rearrange("p j (c i) -> p c j i", i=4)
             if engine == "vector":
                 nc.vector.tensor_copy(dst, src)
             else:
@@ -420,14 +422,14 @@ def tile_list_dispatch_urgency_scores_kernel(
             seats = slice(QUARTER * g, QUARTER * (g + 1))
             nc.vector.quantize_mx(z[1, 0][0][:, seats].bitcast(FP8X4), z[1, 0][1][:, seats], first[g][:])
 
-        sum_in_place(7, 0, slice(0, 1))
-        sum_in_place(7, 0, slice(1, 2))
+        sum_in_place(7, slice(0, 1))
+        sum_in_place(7, slice(1, 2))
         weave("vector", first[0][:], 0, 0)
         weave("scalar", first[1][:], 0, 1)
-        sum_in_place(7, 1, slice(1, 2))
+        sum_in_place(7, slice(3, 4))
         quantize_quarter(0)
         weave("scalar", second[:, 4 * QUARTER :], 1, 1)
-        sum_in_place(7, 1, slice(0, 1))
+        sum_in_place(7, slice(2, 3))
         quantize_quarter(1)
         weave("vector", second[:, 0 : 4 * QUARTER], 1, 0)
         z[1, 1] = quantize(second[:], "z11")

from contextlib import ExitStack

import concourse.mybir as mybir
from concourse.masks import make_identity

K, K2, T, TB, S, PL, H, N = 1024, 512, 4096, 2048, 1024, 512, 1024, 512
FLOPS = 2 * (K * H * S + 2 * K2 * H * PL + 2 * H * N * S)

F32 = mybir.dt.float32
BF16 = mybir.dt.bfloat16
I32 = mybir.dt.int32
U32 = mybir.dt.uint32
U16 = mybir.dt.uint16
U8 = mybir.dt.uint8
FP8X4 = mybir.dt.float8_e4m3fn_x4
FP4X4 = mybir.dt.float4_e2m1fn_x4
ALU = mybir.AluOpType
ACT = mybir.ActivationFunctionType

P = 128
HALF = 512
QUARTER = 256
B2_BANKS = ("b0", "b1", "b2", "b3", "z0", "z1", "b0", "b1")
PAGE_OF = (0, 1, 2, 3, 0, 1, 2, 2)


def tile_list_dispatch_urgency_scores_kernel(
    tc, tab_words, tab_scales, tab2_words, tab2_scales, offs, offs2, pos1,
    w1_words, w1_scales, w2, w3, th, wgs, w4_words, w4_scales, w5, out,
):
    nc = tc.nc
    with ExitStack() as ctx:
        lists = ctx.enter_context(tc.tile_pool(name="lists", bufs=1))
        keep = ctx.enter_context(tc.tile_pool(name="keep", bufs=1))
        ring = ctx.enter_context(tc.tile_pool(name="ring", bufs=2))
        psum = ctx.enter_context(tc.psum_pool(name="psum", bufs=1))

        def kept(shape, dtype, name):
            return keep.tile(shape, dtype, name=name, align_bytes=64)

        def ringed(shape, dtype, tag, bufs):
            return ring.tile(shape, dtype, name=tag, tag=tag, bufs=bufs, align_bytes=64)

        def bank(tag):
            return psum.tile([P, HALF], F32, name=tag, tag=tag)

        def load_list(src, name):
            dst = lists.tile(list(src.shape), U16, name=name)
            nc.sync.dma_start(dst[:], src)
            return dst

        def zeroed_plane(engine, shape, name):
            plane = kept(shape, U8, name)
            engine.memset(plane[:].bitcast(I32), 0)
            return plane

        def load_stacked_scales(queue, plane, src):
            passes = src.shape[0]
            for q in range(4):
                queue.dma_start(
                    plane[32 * q : 32 * q + 4 * passes, :].bitcast(I32),
                    src[:, 4 * q : 4 * q + 4, :].bitcast(I32),
                )

        def words_of(src):
            return src.rearrange("p c i -> p (c i)").bitcast(I32)

        def load_rows(dst, src):
            nc.sync.dma_start(dst[:], src.rearrange("(p j) c -> p j c", j=4))

        def cast(engine, dst, src):
            if engine == "vector":
                nc.vector.tensor_copy(dst, src)
            else:
                nc.scalar.activation(dst, src, ACT.Copy)

        def interleave(engine, dst, src):
            cast(
                engine,
                dst.rearrange("p (c i j) -> p c j i", i=4, j=4),
                src.rearrange("p j (c i) -> p c j i", i=4),
            )

        def quantize(grouped, name):
            width = grouped.shape[1] // 4
            codes = kept([P, width], U32, name + "_codes")
            scales = kept([P, width], U8, name + "_scales")
            nc.vector.quantize_mx(codes[:].bitcast(FP8X4), scales[:], grouped)
            return codes, scales

        tab2_plane = zeroed_plane(nc.vector, [P, TB], "tab2_plane")
        tab_plane = zeroed_plane(nc.gpsimd, [P, T], "tab_plane")
        w1_plane = zeroed_plane(nc.vector, [P, H], "w1_plane")
        w4_plane = zeroed_plane(nc.vector, [P, 2 * N], "w4_plane")
        pages = [kept([P, S], F32, "page0")]
        nc.vector.memset(pages[0][:], 0.0)

        def open_page(tag):
            pages.append(ringed([P, S], F32, tag, 1))
            nc.gpsimd.memset(pages[-1][:], 0.0)

        th_rows = kept([P, P], F32, "th_rows")
        nc.vector.memset(th_rows[:], 0.0)
        ident = kept([P, P], F32, "ident")
        make_identity(nc, ident[:])

        idx2 = load_list(offs2, "idx2")
        chunks = ((0, 128), (128, 128), (256, 256))
        raw_low = {}

        def load_low(c):
            c0, width = chunks[c]
            for m, w in enumerate((w2, w3)):
                raw_low[c, m] = ringed([P, 4, width], F32, f"raw_low{c}_{m}", 1)
                load_rows(raw_low[c, m], w[:, c0 : c0 + width])

        def load_high(w, tag):
            raw = ringed([P, 4, HALF], F32, tag, 1)
            load_rows(raw, w[:, HALF:H])
            return raw

        tab2_sb = ringed([P, TB], U32, "tab2_sb", 1)
        nc.sync.dma_start(tab2_sb[:].bitcast(I32), words_of(tab2_words[0]))
        load_stacked_scales(nc.sync, tab2_plane, tab2_scales)
        load_low(0)
        load_stacked_scales(nc.gpsimd, tab_plane, tab_scales)
        idx = load_list(offs, "idx")
        load_low(1)
        seat = load_list(pos1, "seat")
        wgs_rows = kept([P, PL], F32, "wgs_rows")
        nc.sync.dma_start(wgs_rows[:], wgs)
        tab_sb = [ringed([P, T], U32, f"tab_sb{a}", 1) for a in range(2)]
        load_low(2)
        nc.sync.dma_start(th_rows[0:4, :], th[0:HALF].rearrange("(i p) -> i p", p=P))
        raw_high = [load_high(w2, "raw_w2"), load_high(w3, "raw_w3")]
        nc.sync.dma_start(tab_sb[0][:].bitcast(I32), words_of(tab_words[0]))
        nc.sync.dma_start(tab_sb[1][:].bitcast(I32), words_of(tab_words[1]))
        wgs_dealt = [kept([P, PL], F32, f"wgs_dealt{t}") for t in range(4)]

        def load_dealt(t):
            for q in range(4):
                nc.sync.dma_start(wgs_dealt[t][32 * q : 32 * q + 32, :], wgs.rearrange("(p t) j -> p t j", t=4)[:, t, :])

        def load_w4():
            for q in range(4):
                nc.sync.dma_start(
                    w4_plane[32 * q : 32 * q + 4, :].bitcast(I32).rearrange("r (a n) -> r a n", a=2),
                    w4_scales[:, 4 * q : 4 * q + 4, :].bitcast(I32).rearrange("a r n -> r a n"),
                )
            words = kept([P, 2, 2 * N], U8, "w4_sb")
            nc.sync.dma_start(words[:].bitcast(I32), w4_words.rearrange("a p c -> p a c").bitcast(I32))
            return words

        v2_scales = kept([P, PL], U8, "v2_scales")
        nc.vector.tensor_copy(v2_scales[:], tab2_plane[:].indirect(idx2[:]))
        weights = {}

        def prepare_low(c):
            c0, width = chunks[c]
            grouped = ringed([P, 8 * width], BF16, "grouped", 3)
            for m in range(2):
                engine = "vector" if (c, m) == (0, 1) else "scalar"
                interleave(engine, grouped[:, 4 * width * m : 4 * width * (m + 1)], raw_low[c, m][:])
            codes, scales = quantize(grouped[:], f"w23_low{c}")
            for i in range(width // P):
                for m in range(2):
                    cols = slice(width * m + P * i, width * m + P * (i + 1))
                    weights[c0 // P + i, m] = (codes[:, cols], scales[:, cols])

        def prepare_high():
            for m in range(2):
                grouped = ringed([P, 4 * HALF], BF16, "grouped", 3)
                cast(
                    "scalar",
                    grouped[:].rearrange("p (t q j) -> p q j t", t=4, j=4),
                    raw_high[m][:].rearrange("p j (q t) -> p q j t", t=4),
                )
                codes, scales = quantize(grouped[:], f"w23_high{m}")
                for t in range(4):
                    cols = slice(P * t, P * (t + 1))
                    weights[4 + t, m] = (codes[:, cols], scales[:, cols])

        prepare_low(0)
        v2 = kept([P, PL], U32, "v2")
        nc.vector.tensor_copy(v2[:], tab2_sb[:].indirect(idx2[:]))
        w1_bytes = w1_words.rearrange("a p c i -> p a (c i)")
        w1_low = kept([P, 2, HALF], I32, "w1_low")
        nc.sync.dma_start(w1_low[:], w1_bytes[:, :, 0 : 4 * HALF].bitcast(I32))
        load_stacked_scales(nc.sync, w1_plane, w1_scales)
        raw_w5 = [ringed([P, 4, N], F32, "tab2_sb", 1)]
        load_rows(raw_w5[0], w5[0:HALF, :])
        th_high = kept([P, 4], F32, "th_high")
        nc.sync.dma_start(th_high[:], th[HALF:H].rearrange("(p t) -> p t", t=4))
        w1_high = kept([P, 2, HALF], I32, "w1_high")
        nc.sync.dma_start(w1_high[:], w1_bytes[:, :, 4 * HALF : 4 * H].bitcast(I32))
        smaller = {}
        reused = []
        after_casts = []

        def callback_views(i):
            views = []
            for m in (1, 0):
                acc = bank(f"a{i % 2}" if m else B2_BANKS[i])
                codes, scales = weights[i, m]
                nc.tensor.matmul_mx(
                    acc[:], lhsT=codes.bitcast(FP8X4), lhsT_scale=scales,
                    rhs=v2[:].bitcast(FP8X4), rhs_scale=v2_scales[:], start=True, stop=True,
                )
                views.append(acc)
            if i < 2:
                minus_b3 = ringed([P, PL], F32, ("minus_b3_0", "raw_low2_1")[i], 1)[:]
                smaller[i] = ringed([P, PL], F32, f"minus_b_{i}", 1)[:]
            else:
                minus_b3 = after_casts[(i - 2) // 4][:, (i - 2) % 4, :]
                smaller[i] = reused[1][:, PL * (i - 2) : PL * (i - 1)] if i < 4 else reused[0][:, PL * (i - 4) : PL * (i - 3)]
            nc.scalar.activation(minus_b3, views[0][:], ACT.Copy, scale=-1.0)
            nc.vector.scalar_tensor_tensor(
                smaller[i], views[1][:], -1.0, minus_b3, ALU.mult, ALU.max
            )

        def place(i):
            gain = wgs_rows[:] if i < 4 else wgs_dealt[i - 4][:]
            nc.vector.tensor_tensor(pages[PAGE_OF[i]][:].indirect(seat[:]), smaller[i], gain, ALU.mult)

        callback_views(0)
        open_page("minus_b3_0")
        place(0)
        open_page("minus_b_0")

        prepare_low(1)
        prepare_low(2)
        callback_views(1)
        open_page("raw_low2_1")
        place(1)
        prepare_high()
        after_casts.extend(ringed([P, 4, PL], F32, tag, 1) for tag in ("raw_w3", "raw_w2"))
        v_scales = kept([P, S], U8, "v_scales")
        nc.vector.tensor_copy(v_scales[:], tab_plane[:].indirect(idx[:]))
        v = [kept([P, S], U32, f"v{a}") for a in range(2)]
        for a in range(2):
            nc.vector.tensor_copy(v[a][:], tab_sb[a][:].indirect(idx[:]))
        reused.extend(ringed([P, T], F32, f"tab_sb{a}", 1) for a in range(2))
        minus_th_low = kept([P, 4], F32, "minus_th_low")
        turned = bank("z1")
        nc.tensor.transpose(turned[:, 0:P], th_rows[:], ident[:])
        nc.scalar.activation(minus_th_low[:], turned[:, 0:4], ACT.Copy, scale=-1.0)

        for i in (2, 3):
            callback_views(i)
            place(i)
        for i in range(4, 8):
            callback_views(i)

        w1_dealt = kept([P, 2, HALF], I32, "w1_dealt")
        nc.vector.tensor_copy(
            w1_dealt[:].rearrange("p a (t q i) -> p a q t i", t=4, i=4),
            w1_high[:].rearrange("p a (q i t) -> p a q t i", t=4, i=4),
        )
        w1_plane_dealt = kept([P, HALF], U8, "w1_plane_dealt")
        nc.vector.tensor_copy(
            w1_plane_dealt[:].rearrange("p (t q) -> p t q", t=4),
            w1_plane[:, HALF:H].rearrange("p (q t) -> p t q", t=4),
        )

        load_dealt(0)
        raw_w5.append(ringed([P, 4, N], F32, "raw_w2", 1))
        load_rows(raw_w5[1], w5[HALF:H, :])
        load_dealt(1)
        load_dealt(2)
        w4_sb = load_w4()
        load_dealt(3)

        sizes = {}

        def magnitudes(i, halves=(0, 1)):
            words, plane = (w1_low, w1_plane) if i < 4 else (w1_dealt, w1_plane_dealt)
            cols = slice(P * (i % 4), P * (i % 4 + 1))
            if i not in sizes:
                sizes[i] = reused[(i - 4) // 2][:, S * (2 + i % 2) : S * (3 + i % 2)] if i >= 4 else ringed([P, S], F32, "size", 3)[:]
            size = sizes[i]
            for h in halves:
                seats = slice(HALF * h, HALF * (h + 1))
                acc = bank(f"a{h}")
                for a in range(2):
                    nc.tensor.matmul_mx(
                        acc[:], lhsT=words[:, a, cols].bitcast(FP8X4), lhsT_scale=plane[4 * a :, cols],
                        rhs=v[a][:, seats].bitcast(FP8X4), rhs_scale=v_scales[4 * a :, seats],
                        start=a == 0, stop=a == 1,
                    )
                nc.scalar.activation(size[:, seats], acc[:], ACT.Abs)

        z_turned = [kept([P, 4, HALF], BF16, f"z_turned{h}") for h in range(2)]

        def sum_turned(i, halves):
            size = sizes[i]
            level = minus_th_low[:, i : i + 1].to_broadcast([P, P])
            for h in halves:
                acc = bank(f"z{h}")
                for term in range(3):
                    for b in range(4):
                        seats = slice(HALF * h + P * b, HALF * h + P * (b + 1))
                        src = (size[:, seats], level, pages[i][:, seats])[term]
                        nc.tensor.matmul(
                            acc[:, P * b : P * (b + 1)], lhsT=src, rhs=ident[:], is_transpose=True,
                            start=(term, b) == (0, 0), stop=(term, b) == (2, 3),
                        )
                nc.scalar.copy(
                    z_turned[h][:].rearrange("j b (u q e) -> j b u q e", u=2, e=2)[:, :, :, 32 * i : 32 * (i + 1), :],
                    acc[:].rearrange("j (b q u e) -> j b u q e", b=4, u=2, e=2),
                )

        z = {}

        def quantize_low(halves):
            for h in halves:
                pairs = z_turned[h][:].bitcast(F32)
                grouped = ringed([P, 2 * HALF], F32, "z_grouped", 2)
                for g in range(2):
                    acc = bank(f"z{g}")
                    for b in range(2):
                        for u in range(2):
                            nc.tensor.transpose(
                                acc[:, P * (2 * b + u) : P * (2 * b + u + 1)],
                                pairs[:, 2 * g + b, P * u : P * (u + 1)], ident[:],
                            )
                    nc.scalar.copy(
                        grouped[:, HALF * g : HALF * (g + 1)].rearrange("p (b j u) -> p b j u", b=2, u=2),
                        acc[:].rearrange("p (b u j) -> p b j u", b=2, u=2),
                    )
                z[0, h] = quantize(grouped[:].bitcast(BF16), f"z0{h}")

        z_rows = kept([P, 4, 4, QUARTER], BF16, "z_rows")

        def sum_in_place(i, quarters):
            t = i - 4
            seats = slice(QUARTER * quarters.start, QUARTER * quarters.stop)
            nc.vector.scalar_tensor_tensor(
                z_rows[:, quarters, t, :],
                sizes[i][:, seats].rearrange("p (g j) -> p g j", j=QUARTER),
                th_high[:, t : t + 1],
                pages[PAGE_OF[i]][:, seats].rearrange("p (g j) -> p g j", j=QUARTER),
                ALU.subtract, ALU.add,
            )

        w5_q = []

        def prepare_w5(a, pieces):
            grouped = ringed([P, 4 * N], BF16, "grouped", 3)
            width = N // pieces
            for c0 in range(0, N, width):
                interleave("scalar", grouped[:, 4 * c0 : 4 * (c0 + width)], raw_w5[a][:, :, c0 : c0 + width])
            w5_q.append(quantize(grouped[:], f"w5_{a}"))

        magnitudes(0)
        for i in range(4):
            for h in range(2):
                magnitudes(i + 1, (h,))
                sum_turned(i, (h,))
            if i < 3:
                place(4 + i)
        for a in range(2):
            prepare_w5(a, 4)
        sum_in_place(4, slice(0, 4))
        for h in range(2):
            magnitudes(5, (h,))
            quantize_low((h,))
        sum_in_place(5, slice(0, 4))
        magnitudes(6)
        sum_in_place(6, slice(0, 4))
        place(7)
        magnitudes(7)

        y_banks = (("b0", "b1"), ("b2", "b3"), ("z0", "z1"), ("a0", "a1"))

        def y4_pass(acc, n, h, a, seats, stop):
            codes, scales = z[a, h]
            nc.tensor.matmul_mx(
                acc[:, seats], lhsT=w4_sb[:, a, 2 * P * n : 2 * P * (n + 1)].bitcast(FP4X4),
                lhsT_scale=w4_plane[:, N * a + P * n : N * a + P * (n + 1)],
                rhs=codes[:, seats].bitcast(FP8X4), rhs_scale=scales[:, seats], start=a == 0, stop=stop,
            )

        def y5_pass(acc, n, h, a, seats, stop):
            codes, scales = z[a, h]
            cols = slice(P * n, P * (n + 1))
            nc.tensor.matmul_mx(
                acc[:, seats], lhsT=w5_q[a][0][:, cols].bitcast(FP8X4), lhsT_scale=w5_q[a][1][:, cols],
                rhs=codes[:, seats].bitcast(FP8X4), rhs_scale=scales[:, seats], start=a == 0, stop=stop,
            )

        def finish(acc4, acc5, n, h, pieces):
            y4 = ringed([P, HALF], F32, "y4", 2)
            nc.scalar.copy(y4[:], acc4[:])
            width = HALF // pieces
            result = ringed([P, HALF], F32, "result", 5)
            for c0 in range(0, HALF, width):
                seats = slice(c0, c0 + width)
                nc.vector.tensor_tensor(result[:, seats], acc5[:, seats], y4[:, seats], ALU.mult)
                nc.sync.dma_start(out[P * n : P * (n + 1), HALF * h + c0 : HALF * h + c0 + width], result[:, seats])

        whole = slice(0, HALF)
        early = []
        for n in range(4):
            acc4, acc5 = bank(y_banks[n][0]), bank(y_banks[n][1])
            y4_pass(acc4, n, 0, 0, whole, False)
            y5_pass(acc5, n, 0, 0, whole, False)
            early.append((acc4, acc5))

        def weave(engine, grouped, h, g):
            dst = grouped.rearrange("p (c i j) -> p c j i", i=4, j=4)
            src = z_rows[:, 2 * h + g, :, :].rearrange("p j (c i) -> p c j i", i=4)
            if engine == "vector":
                nc.vector.tensor_copy(dst, src)
            else:
                nc.scalar.copy(dst, src)

        z[1, 0] = (kept([P, HALF], U32, "z10_codes"), kept([P, HALF], U8, "z10_scales"))
        first = [kept([P, 4 * QUARTER], BF16, f"z_quarter{g}") for g in range(2)]
        second = ringed([P, 4 * HALF], BF16, "z_grouped", 2)

        def quantize_quarter(g):
            seats = slice(QUARTER * g, QUARTER * (g + 1))
            nc.vector.quantize_mx(z[1, 0][0][:, seats].bitcast(FP8X4), z[1, 0][1][:, seats], first[g][:])

        sum_in_place(7, slice(0, 1))
        sum_in_place(7, slice(1, 2))
        weave("vector", first[0][:], 0, 0)
        weave("scalar", first[1][:], 0, 1)
        sum_in_place(7, slice(3, 4))
        quantize_quarter(0)
        weave("scalar", second[:, 4 * QUARTER :], 1, 1)
        sum_in_place(7, slice(2, 3))
        quantize_quarter(1)
        weave("vector", second[:, 0 : 4 * QUARTER], 1, 0)
        z[1, 1] = quantize(second[:], "z11")

        for g in range(2):
            for n in range(4):
                acc4, acc5 = early[n]
                for b in range(2):
                    c0 = QUARTER * g + P * b
                    y4_pass(acc4, n, 0, 1, slice(c0, c0 + P), (g, b) == (1, 1))
                y5_pass(acc5, n, 0, 1, slice(QUARTER * g, QUARTER * (g + 1)), g == 1)
                if g == 1:
                    finish(acc4, acc5, n, 0, 1)
        for pair in ((0,), (1,), (2, 3)):
            accs = {n: (bank(y_banks[n][0]), bank(y_banks[n][1])) for n in pair}
            for n in pair:
                for a in range(2):
                    y4_pass(accs[n][0], n, 1, a, whole, a == 1)
            for n in pair:
                for a in range(2):
                    y5_pass(accs[n][1], n, 1, a, whole, a == 1)
                finish(*accs[n], n, 1, 2 if n == 3 else 1)
